import numpy as np
import ml_dtypes


def mxq(x, axis, fmt="e4m3"):
    dtype, down = {"e4m3": (ml_dtypes.float8_e4m3fn, 7), "e5m2": (ml_dtypes.float8_e5m2, 14)}[fmt]
    v = np.moveaxis(np.asarray(x, np.float32).astype(ml_dtypes.bfloat16).astype(np.float64), axis, -1)
    blocks = v.reshape(v.shape[:-1] + (-1, 32))
    amax = np.abs(blocks).max(-1, keepdims=True)
    byte = np.maximum(np.where(amax > 0, np.frexp(amax)[1] - 1 + 127, 0) - down, 1)
    scale = np.exp2(byte - 127.0)
    codes = (blocks / scale).astype(np.float32).astype(dtype).astype(np.float64)
    return np.moveaxis((codes * scale).reshape(v.shape), -1, axis)


WIDE = False


def mx_kscale(k):
    if not WIDE:
        return np.ones(k)
    levels = np.array([10, -10, 5, -5, 0])
    if k % 512:
        return np.exp2(np.random.permutation(np.resize(levels, k // 32))).repeat(32)
    a = np.empty((k // 512, 16))
    for p in range(k // 512):
        a[p, :8] = np.random.permutation(np.resize(levels, 8))
        for g in range(8):
            far = levels[np.abs(levels - a[p, g]) >= 10]
            a[p, g + 8] = far[np.random.randint(len(far))]
    return np.exp2(a.ravel()).repeat(32)


def f64(x):
    return np.asarray(x).astype(np.float64)


def striped(idx):
    return np.tile(idx.reshape(-1, 16).T, (8, 1)).astype(np.uint16)


def unstriped(offs):
    return offs[:16].T.reshape(-1).astype(np.int64)


K, T, E, C, N = 512, 1024, 8, 256, 128


def by_expert(wq, xq):
    return np.concatenate([wq[e].T @ xq[:, e * C:(e + 1) * C] for e in range(E)], axis=1)


def setup_inputs():
    n = np.random.standard_normal
    s = mx_kscale(K)[:, None]
    first = np.random.permutation(np.repeat(np.arange(E), T // E))
    second = (first + 1 + np.random.permutation(np.repeat(np.arange(E - 1), -(-T // (E - 1)))[:T])) % E
    while np.bincount(second, minlength=E).max() != T // E:
        load = np.bincount(second, minlength=E); hi, lo = int(load.argmax()), int(load.argmin())
        t = np.flatnonzero((second == hi) & (first != lo))[0]; second[t] = lo
    slot_token = np.empty(E * C, np.int64); pos = np.empty((2, T), np.int64); fill = np.zeros(E, np.int64)
    place = np.stack([np.random.permutation(C) for _ in range(E)])
    for r, deal in enumerate((first, second)):
        for t in np.random.permutation(T):
            e = deal[t]; j = e * C + place[e, fill[e]]; fill[e] += 1; slot_token[j] = t; pos[r, t] = j
    g = np.random.uniform(0.2, 0.8, T)
    return {
        "xT": (n((K, T)) * s).astype(np.float32),
        "w": (n((E, K, N)) / np.sqrt(K) / s[None]).astype(np.float32),
        "gate": np.stack([np.tile(g, (N, 1)), np.tile(1.0 - g, (N, 1))]).astype(np.float32),
        "offs": striped(slot_token),
        "pos1": striped(pos[0]),
        "pos2": striped(pos[1]),
    }


def reference(xT, w, gate, offs, pos1, pos2):
    idx = unstriped(offs)
    xq = mxq(f64(xT)[:, idx], 0, "e4m3")
    y = by_expert(mxq(f64(w), 1, "e4m3"), xq)
    return f64(gate[0]) * y[:, unstriped(pos1)] + f64(gate[1]) * y[:, unstriped(pos2)]

@@ -1,0 +1,163 @@
+from contextlib import ExitStack
+
+import concourse.mybir as mybir
+
+K, T, E, C, N = 512, 1024, 8, 256, 128
+SLOTS = E * C
+FLOPS = 2 * K * N * SLOTS
+
+F32 = mybir.dt.float32
+BF16 = mybir.dt.bfloat16
+U32 = mybir.dt.uint32
+U16 = mybir.dt.uint16
+U8 = mybir.dt.uint8
+FP8X4 = mybir.dt.float8_e4m3fn_x4
+MULT = mybir.AluOpType.mult
+ADD = mybir.AluOpType.add
+COPY = mybir.ActivationFunctionType.Copy
+
+P = 128
+SLICES = ((0, 1), (2, 3), (4, 5), (6,), (7,))
+SCALAR_UNITS = (0, 1, 2, 3, 4, 5, 6, 7)
+W_ENGINE = "vvvv"
+OUT_ENGINE = "vvvvvvvv"
+CHUNK = 256
+
+
+def tile_routed_moe_kernel(tc, xT, w, gate, offs, pos1, pos2, out):
+    nc = tc.nc
+    with ExitStack() as ctx:
+        lists = ctx.enter_context(tc.tile_pool(name="lists", bufs=1))
+        keep = ctx.enter_context(tc.tile_pool(name="keep", bufs=1))
+        psum = ctx.enter_context(tc.psum_pool(name="psum", bufs=1))
+        copy_on = {"v": nc.vector.tensor_copy, "s": nc.scalar.copy, "g": nc.gpsimd.tensor_copy}
+
+        offs_t = lists.tile([P, SLOTS // 16], U16, name="offs_t")
+        pos1_t = lists.tile([P, T // 16], U16, name="pos1_t")
+        pos2_t = lists.tile([P, T // 16], U16, name="pos2_t")
+
+        nc.sync.dma_start(offs_t[:], offs)
+        planes = xT.rearrange("(p t) n -> t p n", t=4)
+        xr = [keep.tile([P, 2, T], F32, name="xr%d" % u) for u in range(2)]
+        for t in (0, 2, 1, 3):
+            nc.sync.dma_start(xr[t // 2][:, t % 2, :], planes[t])
+        wraw = []
+        for q in range(E // 2):
+            wr = keep.tile([P, 2, 4, N], F32, name="wraw%d" % q)
+            nc.sync.dma_start(wr[:], w[2 * q : 2 * q + 2].rearrange("e (p j) n -> p e j n", j=4))
+            wraw.append(wr)
+        nc.sync.dma_start(pos1_t[:], pos1)
+        nc.sync.dma_start(pos2_t[:], pos2)
+        gate_t = []
+        for r in range(2):
+            g = keep.tile([P, T], F32, name="gate%d" % r)
+            nc.sync.dma_start(g[:], gate[r])
+            gate_t.append(g)
+
+        warm_a = keep.tile([P, 1], F32, name="warm_a")
+        warm_b = keep.tile([P, 1], F32, name="warm_b")
+        nc.vector.memset(warm_a[:], 0.0)
+        nc.scalar.copy(warm_b[:], warm_a[:])
+
+        xb = keep.tile([P, 2, T], BF16, name="xb")
+        grouped, xc, xs, where = [], [], [], {}
+        for i, experts in enumerate(SLICES):
+            n = len(experts) * C
+            grouped.append(keep.tile([P, n, 4], BF16, name="grouped%d" % i, align_bytes=64))
+            xc.append(keep.tile([P, n], U32, name="xc%d" % i, align_bytes=64))
+            xs.append(keep.tile([P, n], U8, name="xs%d" % i, align_bytes=64))
+            for j, e in enumerate(experts):
+                where[e] = (i, j * C)
+        wc = keep.tile([P, E * N], U32, name="wc", align_bytes=64)
+        ws = keep.tile([P, E * N], U8, name="ws", align_bytes=64)
+        wg = [keep.tile([P, 4, N, 4], BF16, name="wg%d" % i, align_bytes=64) for i in range(2)]
+        y = keep.tile([P, SLOTS], F32, name="y")
+        acc = [psum.tile([P, C], F32, name="acc%d" % e) for e in range(E)]
+
+        def cast_plane(t):
+            nc.scalar.copy(xb[:, t - 2, :], xr[1][:, t - 2, :])
+
+        def gather(t, e):
+            i, c0 = where[e]
+            dst = grouped[i][:, c0 : c0 + C, t]
+            entries = offs_t[:, e * (C // 16) : (e + 1) * (C // 16)]
+            if t >= 2 and e in SCALAR_UNITS:
+                nc.scalar.activation(dst, xb[:, t - 2, :].indirect(entries), COPY)
+            else:
+                nc.vector.tensor_copy(dst, xr[t // 2][:, t % 2, :].indirect(entries))
+
+        def interleave_w(q):
+            copy_on[W_ENGINE[q]](
+                wg[q // 2][:, 2 * (q % 2) : 2 * (q % 2) + 2, :, :],
+                wraw[q][:].rearrange("p e j n -> p e n j"),
+            )
+
+        def quantise_w(i):
+            cols = slice(i * 4 * N, (i + 1) * 4 * N)
+            nc.vector.quantize_mx(
+                out=wc[:, cols].bitcast(FP8X4),
+                scales=ws[:, cols],
+                in_=wg[i][:].rearrange("p e n j -> p (e n j)"),
+            )
+
+        def finish_slice(i):
+            nc.vector.quantize_mx(
+                out=xc[i][:].bitcast(FP8X4),
+                scales=xs[i][:],
+                in_=grouped[i][:].rearrange("p n t -> p (n t)"),
+            )
+            for e in SLICES[i]:
+                c0 = where[e][1]
+                nc.tensor.matmul_mx(
+                    out=acc[e][:],
+                    lhsT=wc[:, e * N : (e + 1) * N].bitcast(FP8X4),
+                    lhsT_scale=ws[:, e * N : (e + 1) * N],
+                    rhs=xc[i][:, c0 : c0 + C].bitcast(FP8X4),
+                    rhs_scale=xs[i][:, c0 : c0 + C],
+                    start=True,
+                    stop=True,
+                )
+            for e in SLICES[i]:
+                copy_on[OUT_ENGINE[e]](y[:, e * C : (e + 1) * C], acc[e][:])
+
+        for e in range(4):
+            gather(0, e)
+        cast_plane(2)
+        gather(2, 0)
+        gather(2, 1)
+        cast_plane(3)
+        gather(3, 0)
+        gather(3, 1)
+        for e in range(4):
+            gather(1, e)
+        for e in (2, 3):
+            gather(2, e)
+            gather(3, e)
+        interleave_w(0)
+        interleave_w(1)
+        quantise_w(0)
+        finish_slice(0)
+        for e in (4, 5):
+            for t in range(4):
+                gather(t, e)
+        finish_slice(1)
+        interleave_w(2)
+        interleave_w(3)
+        quantise_w(1)
+        for e in (6, 7):
+            for t in range(4):
+                gather(t, e)
+        finish_slice(2)
+        finish_slice(3)
+        finish_slice(4)
+
+        first = keep.tile([P, T], F32, name="first")
+        second = keep.tile([P, T], F32, name="second")
+        total = keep.tile([P, T], F32, name="total")
+        for c in range(T // CHUNK):
+            cols = slice(c * CHUNK, (c + 1) * CHUNK)
+            lcols = slice(c * CHUNK // 16, (c + 1) * CHUNK // 16)
+            nc.vector.tensor_tensor(first[:, cols], y[:].indirect(pos1_t[:, lcols]), gate_t[0][:, cols], MULT)
+            nc.vector.tensor_tensor(second[:, cols], y[:].indirect(pos2_t[:, lcols]), gate_t[1][:, cols], MULT)
+            nc.vector.tensor_tensor(total[:, cols], first[:, cols], second[:, cols], ADD)
+            nc.sync.dma_start(out[:, cols], total[:, cols])

@@ -20,8 +20,9 @@ P = 128
 SLICES = ((0, 1), (2, 3), (4, 5), (6,), (7,))
 SCALAR_UNITS = (0, 1, 2, 3, 4, 5, 6, 7)
 W_ENGINE = "vvvv"
-OUT_ENGINE = "vvvvvvvv"
-CHUNK = 256
+IL_ENGINE = "ssvvv"
+OUT_ENGINE = "ssssssvs"
+CHUNKS = (256, 256, 256, 256)
 
 
 def tile_routed_moe_kernel(tc, xT, w, gate, offs, pos1, pos2, out):
@@ -60,9 +61,10 @@ def tile_routed_moe_kernel(tc, xT, w, gate, offs, pos1, pos2, out):
         nc.scalar.copy(warm_b[:], warm_a[:])
 
         xb = keep.tile([P, 2, T], BF16, name="xb")
-        grouped, xc, xs, where = [], [], [], {}
+        pairs, grouped, xc, xs, where = [], [], [], [], {}
         for i, experts in enumerate(SLICES):
             n = len(experts) * C
+            pairs.append(keep.tile([P, 2, n, 2], BF16, name="pairs%d" % i, align_bytes=64))
             grouped.append(keep.tile([P, n, 4], BF16, name="grouped%d" % i, align_bytes=64))
             xc.append(keep.tile([P, n], U32, name="xc%d" % i, align_bytes=64))
             xs.append(keep.tile([P, n], U8, name="xs%d" % i, align_bytes=64))
@@ -79,7 +81,7 @@ def tile_routed_moe_kernel(tc, xT, w, gate, offs, pos1, pos2, out):
 
         def gather(t, e):
             i, c0 = where[e]
-            dst = grouped[i][:, c0 : c0 + C, t]
+            dst = pairs[i][:, t // 2, c0 : c0 + C, t % 2]
             entries = offs_t[:, e * (C // 16) : (e + 1) * (C // 16)]
             if t >= 2 and e in SCALAR_UNITS:
                 nc.scalar.activation(dst, xb[:, t - 2, :].indirect(entries), COPY)
@@ -100,12 +102,20 @@ def tile_routed_moe_kernel(tc, xT, w, gate, offs, pos1, pos2, out):
                 in_=wg[i][:].rearrange("p e n j -> p (e n j)"),
             )
 
-        def finish_slice(i):
+        def interleave_x(i):
+            copy_on[IL_ENGINE[i]](
+                grouped[i][:].rearrange("p n t -> p (n t)").bitcast(F32).rearrange("p (n u) -> p n u", u=2),
+                pairs[i][:].rearrange("p u n e -> p (u n e)").bitcast(F32).rearrange("p (u n) -> p n u", u=2),
+            )
+
+        def quantise_x(i):
             nc.vector.quantize_mx(
                 out=xc[i][:].bitcast(FP8X4),
                 scales=xs[i][:],
                 in_=grouped[i][:].rearrange("p n t -> p (n t)"),
             )
+
+        def multiply(i):
             for e in SLICES[i]:
                 c0 = where[e][1]
                 nc.tensor.matmul_mx(
@@ -119,6 +129,11 @@ def tile_routed_moe_kernel(tc, xT, w, gate, offs, pos1, pos2, out):
                 )
             for e in SLICES[i]:
                 copy_on[OUT_ENGINE[e]](y[:, e * C : (e + 1) * C], acc[e][:])
+
+        def finish_slice(i):
+            interleave_x(i)
+            quantise_x(i)
+            multiply(i)
 
         for e in range(4):
             gather(0, e)
@@ -154,10 +169,12 @@ def tile_routed_moe_kernel(tc, xT, w, gate, offs, pos1, pos2, out):
         first = keep.tile([P, T], F32, name="first")
         second = keep.tile([P, T], F32, name="second")
         total = keep.tile([P, T], F32, name="total")
-        for c in range(T // CHUNK):
-            cols = slice(c * CHUNK, (c + 1) * CHUNK)
-            lcols = slice(c * CHUNK // 16, (c + 1) * CHUNK // 16)
+        c0 = 0
+        for chunk in CHUNKS:
+            cols = slice(c0, c0 + chunk)
+            lcols = slice(c0 // 16, (c0 + chunk) // 16)
             nc.vector.tensor_tensor(first[:, cols], y[:].indirect(pos1_t[:, lcols]), gate_t[0][:, cols], MULT)
             nc.vector.tensor_tensor(second[:, cols], y[:].indirect(pos2_t[:, lcols]), gate_t[1][:, cols], MULT)
             nc.vector.tensor_tensor(total[:, cols], first[:, cols], second[:, cols], ADD)
             nc.sync.dma_start(out[:, cols], total[:, cols])
+            c0 += chunk

@@ -17,11 +17,12 @@ ADD = mybir.AluOpType.add
 COPY = mybir.ActivationFunctionType.Copy
 
 P = 128
-SLICES = ((0, 1), (2, 3), (4, 5), (6,), (7,))
-SCALAR_UNITS = (0, 1, 2, 3, 4, 5, 6, 7)
+SLICES = ((0, 1), (2, 3), (4,), (5,), (6,), (7,))
+SCALAR_UNITS = ((1, 0), (1, 1), (1, 2), (1, 3), (1, 4), (1, 5), (1, 6), (1, 7), (0, 4), (0, 5), (0, 6), (0, 7))
+CAST_ENGINE = "vvvv"
 W_ENGINE = "vvvv"
-IL_ENGINE = "ssvvv"
-OUT_ENGINE = "ssssssvs"
+IL_ENGINE = "vvvvvv"
+OUT_ENGINE = "ssssvvvv"
 CHUNKS = (256, 256, 256, 256)
 
 
@@ -40,7 +41,7 @@ def tile_routed_moe_kernel(tc, xT, w, gate, offs, pos1, pos2, out):
         nc.sync.dma_start(offs_t[:], offs)
         planes = xT.rearrange("(p t) n -> t p n", t=4)
         xr = [keep.tile([P, 2, T], F32, name="xr%d" % u) for u in range(2)]
-        for t in (0, 2, 1, 3):
+        for t in (2, 3, 0, 1):
             nc.sync.dma_start(xr[t // 2][:, t % 2, :], planes[t])
         wraw = []
         for q in range(E // 2):
@@ -60,7 +61,7 @@ def tile_routed_moe_kernel(tc, xT, w, gate, offs, pos1, pos2, out):
         nc.vector.memset(warm_a[:], 0.0)
         nc.scalar.copy(warm_b[:], warm_a[:])
 
-        xb = keep.tile([P, 2, T], BF16, name="xb")
+        xb = keep.tile([P, 4, T], BF16, name="xb")
         pairs, grouped, xc, xs, where = [], [], [], [], {}
         for i, experts in enumerate(SLICES):
             n = len(experts) * C
@@ -77,14 +78,14 @@ def tile_routed_moe_kernel(tc, xT, w, gate, offs, pos1, pos2, out):
         acc = [psum.tile([P, C], F32, name="acc%d" % e) for e in range(E)]
 
         def cast_plane(t):
-            nc.scalar.copy(xb[:, t - 2, :], xr[1][:, t - 2, :])
+            copy_on[CAST_ENGINE[t]](xb[:, t, :], xr[t // 2][:, t % 2, :])
 
         def gather(t, e):
             i, c0 = where[e]
             dst = pairs[i][:, t // 2, c0 : c0 + C, t % 2]
             entries = offs_t[:, e * (C // 16) : (e + 1) * (C // 16)]
-            if t >= 2 and e in SCALAR_UNITS:
-                nc.scalar.activation(dst, xb[:, t - 2, :].indirect(entries), COPY)
+            if (t // 2, e) in SCALAR_UNITS:
+                nc.scalar.activation(dst, xb[:, t, :].indirect(entries), COPY)
             else:
                 nc.vector.tensor_copy(dst, xr[t // 2][:, t % 2, :].indirect(entries))
 
@@ -135,36 +136,30 @@ def tile_routed_moe_kernel(tc, xT, w, gate, offs, pos1, pos2, out):
             quantise_x(i)
             multiply(i)
 
-        for e in range(4):
-            gather(0, e)
         cast_plane(2)
-        gather(2, 0)
-        gather(2, 1)
         cast_plane(3)
-        gather(3, 0)
-        gather(3, 1)
+        cast_plane(0)
+        cast_plane(1)
         for e in range(4):
-            gather(1, e)
-        for e in (2, 3):
             gather(2, e)
             gather(3, e)
-        interleave_w(0)
-        interleave_w(1)
+        for e in range(4):
+            gather(0, e)
+        for e in range(4):
+            gather(1, e)
+        for e in range(4, 8):
+            gather(2, e)
+            gather(3, e)
+        for q in range(4):
+            interleave_w(q)
         quantise_w(0)
-        finish_slice(0)
-        for e in (4, 5):
-            for t in range(4):
-                gather(t, e)
-        finish_slice(1)
-        interleave_w(2)
-        interleave_w(3)
         quantise_w(1)
-        for e in (6, 7):
-            for t in range(4):
-                gather(t, e)
-        finish_slice(2)
-        finish_slice(3)
-        finish_slice(4)
+        finish_slice(0)
+        finish_slice(1)
+        for i in range(2, 6):
+            gather(0, i + 2)
+            gather(1, i + 2)
+            finish_slice(i)
 
         first = keep.tile([P, T], F32, name="first")
         second = keep.tile([P, T], F32, name="second")

@@ -19,11 +19,9 @@ COPY = mybir.ActivationFunctionType.Copy
 P = 128
 SLICES = ((0, 1), (2, 3), (4,), (5,), (6,), (7,))
 SCALAR_UNITS = ((1, 0), (1, 1), (1, 2), (1, 3), (1, 4), (1, 5), (1, 6), (1, 7), (0, 4), (0, 5), (0, 6), (0, 7))
-CAST_ENGINE = "vvvv"
-W_ENGINE = "vvvv"
 IL_ENGINE = "vvvvvv"
-OUT_ENGINE = "ssssvvvv"
-CHUNKS = (256, 256, 256, 256)
+OUT_ENGINE = "ssssss"
+CHUNKS = (896, 128)
 
 
 def tile_routed_moe_kernel(tc, xT, w, gate, offs, pos1, pos2, out):
@@ -32,7 +30,7 @@ def tile_routed_moe_kernel(tc, xT, w, gate, offs, pos1, pos2, out):
         lists = ctx.enter_context(tc.tile_pool(name="lists", bufs=1))
         keep = ctx.enter_context(tc.tile_pool(name="keep", bufs=1))
         psum = ctx.enter_context(tc.psum_pool(name="psum", bufs=1))
-        copy_on = {"v": nc.vector.tensor_copy, "s": nc.scalar.copy, "g": nc.gpsimd.tensor_copy}
+        copy_on = {"v": nc.vector.tensor_copy, "s": nc.scalar.copy}
 
         offs_t = lists.tile([P, SLOTS // 16], U16, name="offs_t")
         pos1_t = lists.tile([P, T // 16], U16, name="pos1_t")
@@ -41,12 +39,12 @@ def tile_routed_moe_kernel(tc, xT, w, gate, offs, pos1, pos2, out):
         nc.sync.dma_start(offs_t[:], offs)
         planes = xT.rearrange("(p t) n -> t p n", t=4)
         xr = [keep.tile([P, 2, T], F32, name="xr%d" % u) for u in range(2)]
-        for t in (2, 3, 0, 1):
-            nc.sync.dma_start(xr[t // 2][:, t % 2, :], planes[t])
+        for t, n0, n1 in ((2, 0, 512), (2, 512, 1024), (3, 0, 1024), (0, 0, 1024), (1, 0, 1024)):
+            nc.sync.dma_start(xr[t // 2][:, t % 2, n0:n1], planes[t][:, n0:n1])
         wraw = []
-        for q in range(E // 2):
-            wr = keep.tile([P, 2, 4, N], F32, name="wraw%d" % q)
-            nc.sync.dma_start(wr[:], w[2 * q : 2 * q + 2].rearrange("e (p j) n -> p e j n", j=4))
+        for i in range(2):
+            wr = keep.tile([P, 4, 4, N], F32, name="wraw%d" % i)
+            nc.sync.dma_start(wr[:], w[4 * i : 4 * i + 4].rearrange("e (p j) n -> p e j n", j=4))
             wraw.append(wr)
         nc.sync.dma_start(pos1_t[:], pos1)
         nc.sync.dma_start(pos2_t[:], pos2)
@@ -62,23 +60,23 @@ def tile_routed_moe_kernel(tc, xT, w, gate, offs, pos1, pos2, out):
         nc.scalar.copy(warm_b[:], warm_a[:])
 
         xb = keep.tile([P, 4, T], BF16, name="xb")
-        pairs, grouped, xc, xs, where = [], [], [], [], {}
+        pairs, grouped, xc, xs, acc, where = [], [], [], [], [], {}
         for i, experts in enumerate(SLICES):
             n = len(experts) * C
             pairs.append(keep.tile([P, 2, n, 2], BF16, name="pairs%d" % i, align_bytes=64))
             grouped.append(keep.tile([P, n, 4], BF16, name="grouped%d" % i, align_bytes=64))
             xc.append(keep.tile([P, n], U32, name="xc%d" % i, align_bytes=64))
             xs.append(keep.tile([P, n], U8, name="xs%d" % i, align_bytes=64))
+            acc.append(psum.tile([P, n], F32, name="acc%d" % i))
             for j, e in enumerate(experts):
                 where[e] = (i, j * C)
         wc = keep.tile([P, E * N], U32, name="wc", align_bytes=64)
         ws = keep.tile([P, E * N], U8, name="ws", align_bytes=64)
         wg = [keep.tile([P, 4, N, 4], BF16, name="wg%d" % i, align_bytes=64) for i in range(2)]
         y = keep.tile([P, SLOTS], F32, name="y")
-        acc = [psum.tile([P, C], F32, name="acc%d" % e) for e in range(E)]
 
-        def cast_plane(t):
-            copy_on[CAST_ENGINE[t]](xb[:, t, :], xr[t // 2][:, t % 2, :])
+        def cast_plane(t, n0, n1):
+            nc.vector.tensor_copy(xb[:, t, n0:n1], xr[t // 2][:, t % 2, n0:n1])
 
         def gather(t, e):
             i, c0 = where[e]
@@ -89,11 +87,8 @@ def tile_routed_moe_kernel(tc, xT, w, gate, offs, pos1, pos2, out):
             else:
                 nc.vector.tensor_copy(dst, xr[t // 2][:, t % 2, :].indirect(entries))
 
-        def interleave_w(q):
-            copy_on[W_ENGINE[q]](
-                wg[q // 2][:, 2 * (q % 2) : 2 * (q % 2) + 2, :, :],
-                wraw[q][:].rearrange("p e j n -> p e n j"),
-            )
+        def interleave_w(i):
+            nc.vector.tensor_copy(wg[i][:], wraw[i][:].rearrange("p e j n -> p e n j"))
 
         def quantise_w(i):
             cols = slice(i * 4 * N, (i + 1) * 4 * N)
@@ -120,7 +115,7 @@ def tile_routed_moe_kernel(tc, xT, w, gate, offs, pos1, pos2, out):
             for e in SLICES[i]:
                 c0 = where[e][1]
                 nc.tensor.matmul_mx(
-                    out=acc[e][:],
+                    out=acc[i][:, c0 : c0 + C],
                     lhsT=wc[:, e * N : (e + 1) * N].bitcast(FP8X4),
                     lhsT_scale=ws[:, e * N : (e + 1) * N],
                     rhs=xc[i][:, c0 : c0 + C].bitcast(FP8X4),
@@ -128,18 +123,16 @@ def tile_routed_moe_kernel(tc, xT, w, gate, offs, pos1, pos2, out):
                     start=True,
                     stop=True,
                 )
-            for e in SLICES[i]:
-                copy_on[OUT_ENGINE[e]](y[:, e * C : (e + 1) * C], acc[e][:])
 
-        def finish_slice(i):
-            interleave_x(i)
-            quantise_x(i)
-            multiply(i)
+        def empty(i):
+            e0 = SLICES[i][0]
+            copy_on[OUT_ENGINE[i]](y[:, e0 * C : (e0 + len(SLICES[i])) * C], acc[i][:])
 
-        cast_plane(2)
-        cast_plane(3)
-        cast_plane(0)
-        cast_plane(1)
+        cast_plane(2, 0, 512)
+        cast_plane(2, 512, 1024)
+        cast_plane(3, 0, 1024)
+        cast_plane(0, 0, 1024)
+        cast_plane(1, 0, 1024)
         for e in range(4):
             gather(2, e)
             gather(3, e)
@@ -148,28 +141,44 @@ def tile_routed_moe_kernel(tc, xT, w, gate, offs, pos1, pos2, out):
         for e in range(4):
             gather(1, e)
         for e in range(4, 8):
-            gather(2, e)
-            gather(3, e)
-        for q in range(4):
-            interleave_w(q)
+            for t in (2, 3, 0, 1):
+                gather(t, e)
+        interleave_w(0)
+        interleave_w(1)
         quantise_w(0)
         quantise_w(1)
-        finish_slice(0)
-        finish_slice(1)
+        interleave_x(0)
+        interleave_x(1)
+        quantise_x(0)
+        quantise_x(1)
+        multiply(0)
+        multiply(1)
         for i in range(2, 6):
-            gather(0, i + 2)
-            gather(1, i + 2)
-            finish_slice(i)
+            interleave_x(i)
+            quantise_x(i)
+            multiply(i)
+        for i in range(6):
+            empty(i)
 
         first = keep.tile([P, T], F32, name="first")
         second = keep.tile([P, T], F32, name="second")
         total = keep.tile([P, T], F32, name="total")
+        bounds = []
         c0 = 0
         for chunk in CHUNKS:
-            cols = slice(c0, c0 + chunk)
-            lcols = slice(c0 // 16, (c0 + chunk) // 16)
-            nc.vector.tensor_tensor(first[:, cols], y[:].indirect(pos1_t[:, lcols]), gate_t[0][:, cols], MULT)
-            nc.vector.tensor_tensor(second[:, cols], y[:].indirect(pos2_t[:, lcols]), gate_t[1][:, cols], MULT)
-            nc.vector.tensor_tensor(total[:, cols], first[:, cols], second[:, cols], ADD)
-            nc.sync.dma_start(out[:, cols], total[:, cols])
+            bounds.append((c0, c0 + chunk))
             c0 += chunk
+
+        def fetch(dst, pos_t, r, a, b):
+            nc.vector.tensor_tensor(dst[:, a:b], y[:].indirect(pos_t[:, a // 16 : b // 16]), gate_t[r][:, a:b], MULT)
+
+        def add_and_store(a, b):
+            nc.vector.tensor_tensor(total[:, a:b], first[:, a:b], second[:, a:b], ADD)
+            nc.sync.dma_start(out[:, a:b], total[:, a:b])
+
+        for c, (a, b) in enumerate(bounds):
+            fetch(first, pos1_t, 0, a, b)
+            if c > 0:
+                add_and_store(bounds[c - 1][0], bounds[c - 1][1])
+            fetch(second, pos2_t, 1, a, b)
+        add_and_store(bounds[-1][0], bounds[-1][1])

@@ -17,11 +17,11 @@ ADD = mybir.AluOpType.add
 COPY = mybir.ActivationFunctionType.Copy
 
 P = 128
-SLICES = ((0, 1), (2, 3), (4,), (5,), (6,), (7,))
+SLICES = ((0, 1), (2, 3), (4, 5), (6,), (7,))
 SCALAR_UNITS = ((1, 0), (1, 1), (1, 2), (1, 3), (1, 4), (1, 5), (1, 6), (1, 7), (0, 4), (0, 5), (0, 6), (0, 7))
-IL_ENGINE = "vvvvvv"
-OUT_ENGINE = "ssssss"
-CHUNKS = (896, 128)
+IL_ENGINE = "vvvvv"
+OUT_ENGINE = "sssss"
+CHUNKS = (768, 256)
 
 
 def tile_routed_moe_kernel(tc, xT, w, gate, offs, pos1, pos2, out):
@@ -153,11 +153,16 @@ def tile_routed_moe_kernel(tc, xT, w, gate, offs, pos1, pos2, out):
         quantise_x(1)
         multiply(0)
         multiply(1)
-        for i in range(2, 6):
-            interleave_x(i)
-            quantise_x(i)
-            multiply(i)
-        for i in range(6):
+        interleave_x(2)
+        interleave_x(3)
+        quantise_x(2)
+        multiply(2)
+        quantise_x(3)
+        multiply(3)
+        interleave_x(4)
+        quantise_x(4)
+        multiply(4)
+        for i in range(5):
             empty(i)
 
         first = keep.tile([P, T], F32, name="first")

@@ -17,10 +17,9 @@ ADD = mybir.AluOpType.add
 COPY = mybir.ActivationFunctionType.Copy
 
 P = 128
-SLICES = ((0, 1), (2, 3), (4, 5), (6,), (7,))
-SCALAR_UNITS = ((1, 0), (1, 1), (1, 2), (1, 3), (1, 4), (1, 5), (1, 6), (1, 7), (0, 4), (0, 5), (0, 6), (0, 7))
-IL_ENGINE = "vvvvv"
-OUT_ENGINE = "sssss"
+GROUPS = ((0, 1, 2, 3), (4, 5), (6,), (7,))
+BANKS = ((0, 1), (2, 3), (4, 5), (6,), (7,))
+VECTOR_UNITS = ((1, 0), (0, 0), (0, 1), (0, 2), (0, 3))
 CHUNKS = (768, 256)
 
 
@@ -30,7 +29,6 @@ def tile_routed_moe_kernel(tc, xT, w, gate, offs, pos1, pos2, out):
         lists = ctx.enter_context(tc.tile_pool(name="lists", bufs=1))
         keep = ctx.enter_context(tc.tile_pool(name="keep", bufs=1))
         psum = ctx.enter_context(tc.psum_pool(name="psum", bufs=1))
-        copy_on = {"v": nc.vector.tensor_copy, "s": nc.scalar.copy}
 
         offs_t = lists.tile([P, SLOTS // 16], U16, name="offs_t")
         pos1_t = lists.tile([P, T // 16], U16, name="pos1_t")
@@ -41,11 +39,9 @@ def tile_routed_moe_kernel(tc, xT, w, gate, offs, pos1, pos2, out):
         xr = [keep.tile([P, 2, T], F32, name="xr%d" % u) for u in range(2)]
         for t, n0, n1 in ((2, 0, 512), (2, 512, 1024), (3, 0, 1024), (0, 0, 1024), (1, 0, 1024)):
             nc.sync.dma_start(xr[t // 2][:, t % 2, n0:n1], planes[t][:, n0:n1])
-        wraw = []
+        wraw = keep.tile([P, E, 4, N], F32, name="wraw", tag="raw", align_bytes=64)
         for i in range(2):
-            wr = keep.tile([P, 4, 4, N], F32, name="wraw%d" % i)
-            nc.sync.dma_start(wr[:], w[4 * i : 4 * i + 4].rearrange("e (p j) n -> p e j n", j=4))
-            wraw.append(wr)
+            nc.sync.dma_start(wraw[:, 4 * i : 4 * i + 4], w[4 * i : 4 * i + 4].rearrange("e (p j) n -> p e j n", j=4))
         nc.sync.dma_start(pos1_t[:], pos1)
         nc.sync.dma_start(pos2_t[:], pos2)
         gate_t = []
@@ -60,47 +56,41 @@ def tile_routed_moe_kernel(tc, xT, w, gate, offs, pos1, pos2, out):
         nc.scalar.copy(warm_b[:], warm_a[:])
 
         xb = keep.tile([P, 4, T], BF16, name="xb")
-        pairs, grouped, xc, xs, acc, where = [], [], [], [], [], {}
-        for i, experts in enumerate(SLICES):
+        pairs, xc, xs, where = [], [], [], {}
+        for i, experts in enumerate(GROUPS):
             n = len(experts) * C
             pairs.append(keep.tile([P, 2, n, 2], BF16, name="pairs%d" % i, align_bytes=64))
-            grouped.append(keep.tile([P, n, 4], BF16, name="grouped%d" % i, align_bytes=64))
             xc.append(keep.tile([P, n], U32, name="xc%d" % i, align_bytes=64))
             xs.append(keep.tile([P, n], U8, name="xs%d" % i, align_bytes=64))
-            acc.append(psum.tile([P, n], F32, name="acc%d" % i))
             for j, e in enumerate(experts):
                 where[e] = (i, j * C)
+        acc, bank_of = [], {}
+        for i, experts in enumerate(BANKS):
+            acc.append(psum.tile([P, len(experts) * C], F32, name="acc%d" % i))
+            for j, e in enumerate(experts):
+                bank_of[e] = (i, j * C)
         wc = keep.tile([P, E * N], U32, name="wc", align_bytes=64)
         ws = keep.tile([P, E * N], U8, name="ws", align_bytes=64)
-        wg = [keep.tile([P, 4, N, 4], BF16, name="wg%d" % i, align_bytes=64) for i in range(2)]
+        wg = keep.tile([P, E, N, 4], BF16, name="wg", tag="stage", align_bytes=64)
         y = keep.tile([P, SLOTS], F32, name="y")
+        grouped = []
 
         def cast_plane(t, n0, n1):
-            nc.vector.tensor_copy(xb[:, t, n0:n1], xr[t // 2][:, t % 2, n0:n1])
+            engine = nc.vector if t >= 2 else nc.gpsimd
+            engine.tensor_copy(xb[:, t, n0:n1], xr[t // 2][:, t % 2, n0:n1])
 
         def gather(t, e):
             i, c0 = where[e]
             dst = pairs[i][:, t // 2, c0 : c0 + C, t % 2]
             entries = offs_t[:, e * (C // 16) : (e + 1) * (C // 16)]
-            if (t // 2, e) in SCALAR_UNITS:
-                nc.scalar.activation(dst, xb[:, t, :].indirect(entries), COPY)
-            else:
+            if (t // 2, e) in VECTOR_UNITS:
                 nc.vector.tensor_copy(dst, xr[t // 2][:, t % 2, :].indirect(entries))
-
-        def interleave_w(i):
-            nc.vector.tensor_copy(wg[i][:], wraw[i][:].rearrange("p e j n -> p e n j"))
-
-        def quantise_w(i):
-            cols = slice(i * 4 * N, (i + 1) * 4 * N)
-            nc.vector.quantize_mx(
-                out=wc[:, cols].bitcast(FP8X4),
-                scales=ws[:, cols],
-                in_=wg[i][:].rearrange("p e n j -> p (e n j)"),
-            )
+            else:
+                nc.scalar.activation(dst, xb[:, t, :].indirect(entries), COPY)
 
         def interleave_x(i):
-            copy_on[IL_ENGINE[i]](
-                grouped[i][:].rearrange("p n t -> p (n t)").bitcast(F32).rearrange("p (n u) -> p n u", u=2),
+            nc.vector.tensor_copy(
+                grouped[i].rearrange("p n t -> p (n t)").bitcast(F32).rearrange("p (n u) -> p n u", u=2),
                 pairs[i][:].rearrange("p u n e -> p (u n e)").bitcast(F32).rearrange("p (u n) -> p n u", u=2),
             )
 
@@ -108,14 +98,15 @@ def tile_routed_moe_kernel(tc, xT, w, gate, offs, pos1, pos2, out):
             nc.vector.quantize_mx(
                 out=xc[i][:].bitcast(FP8X4),
                 scales=xs[i][:],
-                in_=grouped[i][:].rearrange("p n t -> p (n t)"),
+                in_=grouped[i].rearrange("p n t -> p (n t)"),
             )
 
         def multiply(i):
-            for e in SLICES[i]:
+            for e in GROUPS[i]:
                 c0 = where[e][1]
+                b, a0 = bank_of[e]
                 nc.tensor.matmul_mx(
-                    out=acc[i][:, c0 : c0 + C],
+                    out=acc[b][:, a0 : a0 + C],
                     lhsT=wc[:, e * N : (e + 1) * N].bitcast(FP8X4),
                     lhsT_scale=ws[:, e * N : (e + 1) * N],
                     rhs=xc[i][:, c0 : c0 + C].bitcast(FP8X4),
@@ -124,46 +115,43 @@ def tile_routed_moe_kernel(tc, xT, w, gate, offs, pos1, pos2, out):
                     stop=True,
                 )
 
-        def empty(i):
-            e0 = SLICES[i][0]
-            copy_on[OUT_ENGINE[i]](y[:, e0 * C : (e0 + len(SLICES[i])) * C], acc[i][:])
+        def empty(b):
+            e0 = BANKS[b][0]
+            nc.scalar.copy(y[:, e0 * C : (e0 + len(BANKS[b])) * C], acc[b][:])
 
         cast_plane(2, 0, 512)
         cast_plane(2, 512, 1024)
         cast_plane(3, 0, 1024)
-        cast_plane(0, 0, 1024)
-        cast_plane(1, 0, 1024)
-        for e in range(4):
-            gather(2, e)
-            gather(3, e)
-        for e in range(4):
-            gather(0, e)
-        for e in range(4):
-            gather(1, e)
-        for e in range(4, 8):
-            for t in (2, 3, 0, 1):
+        cast_plane(0, 0, 512)
+        cast_plane(0, 512, 1024)
+        cast_plane(1, 0, 512)
+        cast_plane(1, 512, 1024)
+        for t in (2, 3, 0, 1):
+            for e in range(8):
                 gather(t, e)
-        interleave_w(0)
-        interleave_w(1)
-        quantise_w(0)
-        quantise_w(1)
+
+        nc.vector.tensor_copy(wg[:], wraw[:].rearrange("p e j n -> p e n j"))
+        first_group = keep.tile([P, 4 * C, 4], BF16, name="first_group", tag="raw", align_bytes=64)
+        grouped.append(first_group[:])
         interleave_x(0)
-        interleave_x(1)
+        nc.vector.quantize_mx(out=wc[:].bitcast(FP8X4), scales=ws[:], in_=wg[:].rearrange("p e n j -> p (e n j)"))
+        later_groups = keep.tile([P, 4 * C, 4], BF16, name="later_groups", tag="stage", align_bytes=64)
+        for experts in GROUPS[1:]:
+            a = (experts[0] - 4) * C
+            grouped.append(later_groups[:, a : a + len(experts) * C, :])
         quantise_x(0)
-        quantise_x(1)
         multiply(0)
-        multiply(1)
+        interleave_x(1)
         interleave_x(2)
-        interleave_x(3)
+        quantise_x(1)
+        multiply(1)
         quantise_x(2)
         multiply(2)
+        interleave_x(3)
         quantise_x(3)
         multiply(3)
-        interleave_x(4)
-        quantise_x(4)
-        multiply(4)
-        for i in range(5):
-            empty(i)
+        for b in range(len(BANKS)):
+            empty(b)
 
         first = keep.tile([P, T], F32, name="first")
         second = keep.tile([P, T], F32, name="second")

@@ -39,9 +39,12 @@ def tile_routed_moe_kernel(tc, xT, w, gate, offs, pos1, pos2, out):
         xr = [keep.tile([P, 2, T], F32, name="xr%d" % u) for u in range(2)]
         for t, n0, n1 in ((2, 0, 512), (2, 512, 1024), (3, 0, 1024), (0, 0, 1024), (1, 0, 1024)):
             nc.sync.dma_start(xr[t // 2][:, t % 2, n0:n1], planes[t][:, n0:n1])
-        wraw = keep.tile([P, E, 4, N], F32, name="wraw", tag="raw", align_bytes=64)
+        wraw = [
+            keep.tile([P, 4, 4, N], F32, name="wraw0", align_bytes=64),
+            keep.tile([P, 4, 4, N], F32, name="wraw1", tag="raw", align_bytes=64),
+        ]
         for i in range(2):
-            nc.sync.dma_start(wraw[:, 4 * i : 4 * i + 4], w[4 * i : 4 * i + 4].rearrange("e (p j) n -> p e j n", j=4))
+            nc.sync.dma_start(wraw[i][:], w[4 * i : 4 * i + 4].rearrange("e (p j) n -> p e j n", j=4))
         nc.sync.dma_start(pos1_t[:], pos1)
         nc.sync.dma_start(pos2_t[:], pos2)
         gate_t = []
@@ -56,11 +59,12 @@ def tile_routed_moe_kernel(tc, xT, w, gate, offs, pos1, pos2, out):
         nc.scalar.copy(warm_b[:], warm_a[:])
 
         xb = keep.tile([P, 4, T], BF16, name="xb")
-        pairs, xc, xs, where = [], [], [], {}
+        pairs, xc, xs, where = [], {}, [], {}
         for i, experts in enumerate(GROUPS):
             n = len(experts) * C
             pairs.append(keep.tile([P, 2, n, 2], BF16, name="pairs%d" % i, align_bytes=64))
-            xc.append(keep.tile([P, n], U32, name="xc%d" % i, align_bytes=64))
+            if i > 0:
+                xc[i] = keep.tile([P, n], U32, name="xc%d" % i, align_bytes=64)
             xs.append(keep.tile([P, n], U8, name="xs%d" % i, align_bytes=64))
             for j, e in enumerate(experts):
                 where[e] = (i, j * C)
@@ -130,16 +134,19 @@ def tile_routed_moe_kernel(tc, xT, w, gate, offs, pos1, pos2, out):
             for e in range(8):
                 gather(t, e)
 
-        nc.vector.tensor_copy(wg[:], wraw[:].rearrange("p e j n -> p e n j"))
-        first_group = keep.tile([P, 4 * C, 4], BF16, name="first_group", tag="raw", align_bytes=64)
+        for e in range(4):
+            nc.gpsimd.tensor_copy(wg[:, e], wraw[0][:, e].rearrange("p j n -> p n j"))
+        first_group = keep.tile([P, 4 * C, 4], BF16, name="first_group", align_bytes=64)
         grouped.append(first_group[:])
         interleave_x(0)
+        nc.vector.tensor_copy(wg[:, 4:8], wraw[1][:].rearrange("p e j n -> p e n j"))
+        xc[0] = keep.tile([P, 4 * C], U32, name="xc0", tag="raw", align_bytes=64)
+        quantise_x(0)
         nc.vector.quantize_mx(out=wc[:].bitcast(FP8X4), scales=ws[:], in_=wg[:].rearrange("p e n j -> p (e n j)"))
         later_groups = keep.tile([P, 4 * C, 4], BF16, name="later_groups", tag="stage", align_bytes=64)
         for experts in GROUPS[1:]:
             a = (experts[0] - 4) * C
             grouped.append(later_groups[:, a : a + len(experts) * C, :])
-        quantise_x(0)
         multiply(0)
         interleave_x(1)
         interleave_x(2)

@@ -17,7 +17,7 @@ ADD = mybir.AluOpType.add
 COPY = mybir.ActivationFunctionType.Copy
 
 P = 128
-GROUPS = ((0, 1, 2, 3), (4, 5), (6,), (7,))
+GROUPS = ((0, 1, 2, 3), (4,), (5,), (6,), (7,))
 BANKS = ((0, 1), (2, 3), (4, 5), (6,), (7,))
 VECTOR_UNITS = ((1, 0), (0, 0), (0, 1), (0, 2), (0, 3))
 CHUNKS = (768, 256)
@@ -139,7 +139,10 @@ def tile_routed_moe_kernel(tc, xT, w, gate, offs, pos1, pos2, out):
         first_group = keep.tile([P, 4 * C, 4], BF16, name="first_group", align_bytes=64)
         grouped.append(first_group[:])
         interleave_x(0)
-        nc.vector.tensor_copy(wg[:, 4:8], wraw[1][:].rearrange("p e j n -> p e n j"))
+        nc.vector.tensor_copy(
+            wg[:, 4:8].rearrange("p e (c i) j -> p e c j i", i=4),
+            wraw[1][:].rearrange("p e j (c i) -> p e c j i", i=4),
+        )
         xc[0] = keep.tile([P, 4 * C], U32, name="xc0", tag="raw", align_bytes=64)
         quantise_x(0)
         nc.vector.quantize_mx(out=wc[:].bitcast(FP8X4), scales=ws[:], in_=wg[:].rearrange("p e n j -> p (e n j)"))
@@ -149,14 +152,12 @@ def tile_routed_moe_kernel(tc, xT, w, gate, offs, pos1, pos2, out):
             grouped.append(later_groups[:, a : a + len(experts) * C, :])
         multiply(0)
         interleave_x(1)
-        interleave_x(2)
-        quantise_x(1)
-        multiply(1)
-        quantise_x(2)
-        multiply(2)
-        interleave_x(3)
-        quantise_x(3)
-        multiply(3)
+        for i in range(2, len(GROUPS)):
+            interleave_x(i)
+            quantise_x(i - 1)
+            multiply(i - 1)
+        quantise_x(len(GROUPS) - 1)
+        multiply(len(GROUPS) - 1)
         for b in range(len(BANKS)):
             empty(b)
 

@@ -20,6 +20,7 @@ P = 128
 GROUPS = ((0, 1, 2, 3), (4,), (5,), (6,), (7,))
 BANKS = ((0, 1), (2, 3), (4, 5), (6,), (7,))
 VECTOR_UNITS = ((1, 0), (0, 0), (0, 1), (0, 2), (0, 3))
+SHARED_UNITS = ((1, 1),)
 CHUNKS = (768, 256)
 
 
@@ -37,7 +38,7 @@ def tile_routed_moe_kernel(tc, xT, w, gate, offs, pos1, pos2, out):
         nc.sync.dma_start(offs_t[:], offs)
         planes = xT.rearrange("(p t) n -> t p n", t=4)
         xr = [keep.tile([P, 2, T], F32, name="xr%d" % u) for u in range(2)]
-        for t, n0, n1 in ((2, 0, 512), (2, 512, 1024), (3, 0, 1024), (0, 0, 1024), (1, 0, 1024)):
+        for t, n0, n1 in ((2, 0, 256), (2, 256, 512), (2, 512, 768), (2, 768, 1024), (3, 0, 1024), (0, 0, 1024), (1, 0, 1024)):
             nc.sync.dma_start(xr[t // 2][:, t % 2, n0:n1], planes[t][:, n0:n1])
         wraw = [
             keep.tile([P, 4, 4, N], F32, name="wraw0", align_bytes=64),
@@ -80,17 +81,24 @@ def tile_routed_moe_kernel(tc, xT, w, gate, offs, pos1, pos2, out):
         grouped = []
 
         def cast_plane(t, n0, n1):
-            engine = nc.vector if t >= 2 else nc.gpsimd
-            engine.tensor_copy(xb[:, t, n0:n1], xr[t // 2][:, t % 2, n0:n1])
+            if t == 2:
+                nc.scalar.copy(xb[:, t, n0:n1], xr[t // 2][:, t % 2, n0:n1])
+            else:
+                nc.gpsimd.tensor_copy(xb[:, t, n0:n1], xr[t // 2][:, t % 2, n0:n1])
 
         def gather(t, e):
             i, c0 = where[e]
-            dst = pairs[i][:, t // 2, c0 : c0 + C, t % 2]
-            entries = offs_t[:, e * (C // 16) : (e + 1) * (C // 16)]
-            if (t // 2, e) in VECTOR_UNITS:
-                nc.vector.tensor_copy(dst, xr[t // 2][:, t % 2, :].indirect(entries))
+            if (t // 2, e) in SHARED_UNITS:
+                pieces = ((0, C // 2, True), (C // 2, C, False))
             else:
-                nc.scalar.activation(dst, xb[:, t, :].indirect(entries), COPY)
+                pieces = ((0, C, (t // 2, e) in VECTOR_UNITS),)
+            for a, b, on_vector in pieces:
+                dst = pairs[i][:, t // 2, c0 + a : c0 + b, t % 2]
+                entries = offs_t[:, (e * C + a) // 16 : (e * C + b) // 16]
+                if on_vector:
+                    nc.vector.tensor_copy(dst, xr[t // 2][:, t % 2, :].indirect(entries))
+                else:
+                    nc.scalar.activation(dst, xb[:, t, :].indirect(entries), COPY)
 
         def interleave_x(i):
             nc.vector.tensor_copy(
@@ -123,13 +131,11 @@ def tile_routed_moe_kernel(tc, xT, w, gate, offs, pos1, pos2, out):
             e0 = BANKS[b][0]
             nc.scalar.copy(y[:, e0 * C : (e0 + len(BANKS[b])) * C], acc[b][:])
 
-        cast_plane(2, 0, 512)
-        cast_plane(2, 512, 1024)
-        cast_plane(3, 0, 1024)
-        cast_plane(0, 0, 512)
-        cast_plane(0, 512, 1024)
-        cast_plane(1, 0, 512)
-        cast_plane(1, 512, 1024)
+        for n0 in range(0, T, 256):
+            cast_plane(2, n0, n0 + 256)
+        for t in (3, 0, 1):
+            cast_plane(t, 0, 512)
+            cast_plane(t, 512, 1024)
         for t in (2, 3, 0, 1):
             for e in range(8):
                 gather(t, e)

@@ -35,11 +35,12 @@ def tile_routed_moe_kernel(tc, xT, w, gate, offs, pos1, pos2, out):
         pos1_t = lists.tile([P, T // 16], U16, name="pos1_t")
         pos2_t = lists.tile([P, T // 16], U16, name="pos2_t")
 
-        nc.sync.dma_start(offs_t[:], offs)
         planes = xT.rearrange("(p t) n -> t p n", t=4)
         xr = [keep.tile([P, 2, T], F32, name="xr%d" % u) for u in range(2)]
         for t, n0, n1 in ((2, 0, 256), (2, 256, 512), (2, 512, 768), (2, 768, 1024), (3, 0, 1024), (0, 0, 1024), (1, 0, 1024)):
             nc.sync.dma_start(xr[t // 2][:, t % 2, n0:n1], planes[t][:, n0:n1])
+            if (t, n1) == (2, T):
+                nc.sync.dma_start(offs_t[:], offs)
         wraw = [
             keep.tile([P, 4, 4, N], F32, name="wraw0", align_bytes=64),
             keep.tile([P, 4, 4, N], F32, name="wraw1", tag="raw", align_bytes=64),
@@ -101,7 +102,8 @@ def tile_routed_moe_kernel(tc, xT, w, gate, offs, pos1, pos2, out):
                     nc.scalar.activation(dst, xb[:, t, :].indirect(entries), COPY)
 
         def interleave_x(i):
-            nc.vector.tensor_copy(
+            copy = nc.scalar.copy if i == len(GROUPS) - 1 else nc.vector.tensor_copy
+            copy(
                 grouped[i].rearrange("p n t -> p (n t)").bitcast(F32).rearrange("p (n u) -> p n u", u=2),
                 pairs[i][:].rearrange("p u n e -> p (u n e)").bitcast(F32).rearrange("p (u n) -> p n u", u=2),
             )
@@ -134,14 +136,13 @@ def tile_routed_moe_kernel(tc, xT, w, gate, offs, pos1, pos2, out):
         for n0 in range(0, T, 256):
             cast_plane(2, n0, n0 + 256)
         for t in (3, 0, 1):
-            cast_plane(t, 0, 512)
-            cast_plane(t, 512, 1024)
+            cast_plane(t, 0, 1024)
         for t in (2, 3, 0, 1):
             for e in range(8):
                 gather(t, e)
 
-        for e in range(4):
-            nc.gpsimd.tensor_copy(wg[:, e], wraw[0][:, e].rearrange("p j n -> p n j"))
+        for e in (0, 2):
+            nc.gpsimd.tensor_copy(wg[:, e : e + 2], wraw[0][:, e : e + 2].rearrange("p e j n -> p e n j"))
         first_group = keep.tile([P, 4 * C, 4], BF16, name="first_group", align_bytes=64)
         grouped.append(first_group[:])
         interleave_x(0)

@@ -37,16 +37,22 @@ def tile_routed_moe_kernel(tc, xT, w, gate, offs, pos1, pos2, out):
 
         planes = xT.rearrange("(p t) n -> t p n", t=4)
         xr = [keep.tile([P, 2, T], F32, name="xr%d" % u) for u in range(2)]
-        for t, n0, n1 in ((2, 0, 256), (2, 256, 512), (2, 512, 768), (2, 768, 1024), (3, 0, 1024), (0, 0, 1024), (1, 0, 1024)):
-            nc.sync.dma_start(xr[t // 2][:, t % 2, n0:n1], planes[t][:, n0:n1])
-            if (t, n1) == (2, T):
-                nc.sync.dma_start(offs_t[:], offs)
         wraw = [
             keep.tile([P, 4, 4, N], F32, name="wraw0", align_bytes=64),
             keep.tile([P, 4, 4, N], F32, name="wraw1", tag="raw", align_bytes=64),
         ]
-        for i in range(2):
-            nc.sync.dma_start(wraw[i][:], w[4 * i : 4 * i + 4].rearrange("e (p j) n -> p e j n", j=4))
+
+        def load_w(e0, e1):
+            nc.sync.dma_start(wraw[e0 // 4][:, e0 % 4 : e0 % 4 + e1 - e0], w[e0:e1].rearrange("e (p j) n -> p e j n", j=4))
+
+        for t, n0, n1 in ((2, 0, 256), (2, 256, 512), (2, 512, 768), (2, 768, 1024), (3, 0, 1024), (0, 0, 1024), (1, 0, 1024)):
+            if t == 1:
+                load_w(0, 2)
+            nc.sync.dma_start(xr[t // 2][:, t % 2, n0:n1], planes[t][:, n0:n1])
+            if (t, n1) == (2, T):
+                nc.sync.dma_start(offs_t[:], offs)
+        load_w(2, 4)
+        load_w(4, 8)
         nc.sync.dma_start(pos1_t[:], pos1)
         nc.sync.dma_start(pos2_t[:], pos2)
         gate_t = []
@@ -102,8 +108,7 @@ def tile_routed_moe_kernel(tc, xT, w, gate, offs, pos1, pos2, out):
                     nc.scalar.activation(dst, xb[:, t, :].indirect(entries), COPY)
 
         def interleave_x(i):
-            copy = nc.scalar.copy if i == len(GROUPS) - 1 else nc.vector.tensor_copy
-            copy(
+            nc.vector.tensor_copy(
                 grouped[i].rearrange("p n t -> p (n t)").bitcast(F32).rearrange("p (n u) -> p n u", u=2),
                 pairs[i][:].rearrange("p u n e -> p (u n e)").bitcast(F32).rearrange("p (u n) -> p n u", u=2),
             )
@@ -135,14 +140,18 @@ def tile_routed_moe_kernel(tc, xT, w, gate, offs, pos1, pos2, out):
 
         for n0 in range(0, T, 256):
             cast_plane(2, n0, n0 + 256)
-        for t in (3, 0, 1):
-            cast_plane(t, 0, 1024)
+        def copy_w(e):
+            nc.gpsimd.tensor_copy(wg[:, e : e + 2], wraw[0][:, e : e + 2].rearrange("p e j n -> p e n j"))
+
+        cast_plane(3, 0, 1024)
+        cast_plane(0, 0, 1024)
+        copy_w(0)
+        cast_plane(1, 0, 1024)
+        copy_w(2)
         for t in (2, 3, 0, 1):
             for e in range(8):
                 gather(t, e)
 
-        for e in (0, 2):
-            nc.gpsimd.tensor_copy(wg[:, e : e + 2], wraw[0][:, e : e + 2].rearrange("p e j n -> p e n j"))
         first_group = keep.tile([P, 4 * C, 4], BF16, name="first_group", align_bytes=64)
         grouped.append(first_group[:])
         interleave_x(0)

@@ -1,6 +1,7 @@
 from contextlib import ExitStack
 
 import concourse.mybir as mybir
+from concourse.masks import make_identity
 
 K, T, E, C, N = 512, 1024, 8, 256, 128
 SLOTS = E * C
@@ -21,7 +22,8 @@ GROUPS = ((0, 1, 2, 3), (4,), (5,), (6,), (7,))
 BANKS = ((0, 1), (2, 3), (4, 5), (6,), (7,))
 VECTOR_UNITS = ((1, 0), (0, 0), (0, 1), (0, 2), (0, 3))
 SHARED_UNITS = ((1, 1),)
-CHUNKS = (768, 256)
+PE_TOKENS = 384
+LAST = 256
 
 
 def tile_routed_moe_kernel(tc, xT, w, gate, offs, pos1, pos2, out):
@@ -65,6 +67,8 @@ def tile_routed_moe_kernel(tc, xT, w, gate, offs, pos1, pos2, out):
         warm_b = keep.tile([P, 1], F32, name="warm_b")
         nc.vector.memset(warm_a[:], 0.0)
         nc.scalar.copy(warm_b[:], warm_a[:])
+        identity = keep.tile([P, P], F32, name="identity")
+        make_identity(nc, identity[:])
 
         xb = keep.tile([P, 4, T], BF16, name="xb")
         pairs, xc, xs, where = [], {}, [], {}
@@ -180,11 +184,7 @@ def tile_routed_moe_kernel(tc, xT, w, gate, offs, pos1, pos2, out):
         first = keep.tile([P, T], F32, name="first")
         second = keep.tile([P, T], F32, name="second")
         total = keep.tile([P, T], F32, name="total")
-        bounds = []
-        c0 = 0
-        for chunk in CHUNKS:
-            bounds.append((c0, c0 + chunk))
-            c0 += chunk
+        sums = psum.tile([P, PE_TOKENS], F32, name="sums")
 
         def fetch(dst, pos_t, r, a, b):
             nc.vector.tensor_tensor(dst[:, a:b], y[:].indirect(pos_t[:, a // 16 : b // 16]), gate_t[r][:, a:b], MULT)
@@ -193,9 +193,14 @@ def tile_routed_moe_kernel(tc, xT, w, gate, offs, pos1, pos2, out):
             nc.vector.tensor_tensor(total[:, a:b], first[:, a:b], second[:, a:b], ADD)
             nc.sync.dma_start(out[:, a:b], total[:, a:b])
 
-        for c, (a, b) in enumerate(bounds):
-            fetch(first, pos1_t, 0, a, b)
-            if c > 0:
-                add_and_store(bounds[c - 1][0], bounds[c - 1][1])
-            fetch(second, pos2_t, 1, a, b)
-        add_and_store(bounds[-1][0], bounds[-1][1])
+        fetch(first, pos1_t, 0, 0, PE_TOKENS)
+        fetch(second, pos2_t, 1, 0, PE_TOKENS)
+        nc.tensor.matmul(sums[:], identity[:], first[:, 0:PE_TOKENS], start=True, stop=False)
+        nc.tensor.matmul(sums[:], identity[:], second[:, 0:PE_TOKENS], start=False, stop=True)
+        nc.scalar.copy(total[:, 0:PE_TOKENS], sums[:])
+        nc.scalar.dma_start(out[:, 0:PE_TOKENS], total[:, 0:PE_TOKENS])
+        fetch(first, pos1_t, 0, PE_TOKENS, T)
+        fetch(second, pos2_t, 1, PE_TOKENS, T - LAST)
+        fetch(second, pos2_t, 1, T - LAST, T)
+        add_and_store(PE_TOKENS, T - LAST)
+        add_and_store(T - LAST, T)

@@ -23,6 +23,7 @@ BANKS = ((0, 1), (2, 3), (4, 5), (6,), (7,))
 VECTOR_UNITS = ((1, 0), (0, 0), (0, 1), (0, 2), (0, 3))
 SHARED_UNITS = ((1, 1),)
 PE_TOKENS = 384
+PE_HALVES = ((0, 192), (192, 384))
 LAST = 256
 
 
@@ -184,7 +185,7 @@ def tile_routed_moe_kernel(tc, xT, w, gate, offs, pos1, pos2, out):
         first = keep.tile([P, T], F32, name="first")
         second = keep.tile([P, T], F32, name="second")
         total = keep.tile([P, T], F32, name="total")
-        sums = psum.tile([P, PE_TOKENS], F32, name="sums")
+        sums = [psum.tile([P, b - a], F32, name="sums%d" % a) for a, b in PE_HALVES]
 
         def fetch(dst, pos_t, r, a, b):
             nc.vector.tensor_tensor(dst[:, a:b], y[:].indirect(pos_t[:, a // 16 : b // 16]), gate_t[r][:, a:b], MULT)
@@ -195,10 +196,12 @@ def tile_routed_moe_kernel(tc, xT, w, gate, offs, pos1, pos2, out):
 
         fetch(first, pos1_t, 0, 0, PE_TOKENS)
         fetch(second, pos2_t, 1, 0, PE_TOKENS)
-        nc.tensor.matmul(sums[:], identity[:], first[:, 0:PE_TOKENS], start=True, stop=False)
-        nc.tensor.matmul(sums[:], identity[:], second[:, 0:PE_TOKENS], start=False, stop=True)
-        nc.scalar.copy(total[:, 0:PE_TOKENS], sums[:])
-        nc.scalar.dma_start(out[:, 0:PE_TOKENS], total[:, 0:PE_TOKENS])
+        for half, (a, b) in zip(sums, PE_HALVES):
+            nc.tensor.matmul(half[:], identity[:], first[:, a:b], start=True, stop=False)
+        for half, (a, b) in zip(sums, PE_HALVES):
+            nc.tensor.matmul(half[:], identity[:], second[:, a:b], start=False, stop=True)
+            nc.scalar.copy(total[:, a:b], half[:])
+            nc.scalar.dma_start(out[:, a:b], total[:, a:b])
         fetch(first, pos1_t, 0, PE_TOKENS, T)
         fetch(second, pos2_t, 1, PE_TOKENS, T - LAST)
         fetch(second, pos2_t, 1, T - LAST, T)

@@ -48,7 +48,7 @@ def tile_routed_moe_kernel(tc, xT, w, gate, offs, pos1, pos2, out):
         def load_w(e0, e1):
             nc.sync.dma_start(wraw[e0 // 4][:, e0 % 4 : e0 % 4 + e1 - e0], w[e0:e1].rearrange("e (p j) n -> p e j n", j=4))
 
-        for t, n0, n1 in ((2, 0, 256), (2, 256, 512), (2, 512, 768), (2, 768, 1024), (3, 0, 1024), (0, 0, 1024), (1, 0, 1024)):
+        for t, n0, n1 in ((2, 0, 512), (2, 512, 1024), (3, 0, 512), (3, 512, 1024), (0, 0, 1024), (1, 0, 1024)):
             if t == 1:
                 load_w(0, 2)
             nc.sync.dma_start(xr[t // 2][:, t % 2, n0:n1], planes[t][:, n0:n1])
@@ -143,12 +143,14 @@ def tile_routed_moe_kernel(tc, xT, w, gate, offs, pos1, pos2, out):
             e0 = BANKS[b][0]
             nc.scalar.copy(y[:, e0 * C : (e0 + len(BANKS[b])) * C], acc[b][:])
 
-        for n0 in range(0, T, 256):
-            cast_plane(2, n0, n0 + 256)
+        cast_plane(2, 0, 512)
+        cast_plane(2, 512, 768)
+        nc.vector.tensor_copy(xb[:, 2, 768:T], xr[1][:, 0, 768:T])
         def copy_w(e):
             nc.gpsimd.tensor_copy(wg[:, e : e + 2], wraw[0][:, e : e + 2].rearrange("p e j n -> p e n j"))
 
-        cast_plane(3, 0, 1024)
+        for n0 in range(0, T, 512):
+            cast_plane(3, n0, n0 + 512)
         cast_plane(0, 0, 1024)
         copy_w(0)
         cast_plane(1, 0, 1024)

@@ -19,9 +19,9 @@ COPY = mybir.ActivationFunctionType.Copy
 
 P = 128
 GROUPS = ((0, 1, 2, 3), (4,), (5,), (6,), (7,))
-BANKS = ((0, 1), (2, 3), (4, 5), (6,), (7,))
-VECTOR_UNITS = ((1, 0), (0, 0), (0, 1), (0, 2), (0, 3))
-SHARED_UNITS = ((1, 1),)
+BANKS = ((0, 512), (512, 1024), (1024, 1536), (1536, 1792), (1792, 1920), (1920, 2048))
+VECTOR_BANKS = (2,)
+VECTOR_UNITS = ((1, 0), (1, 1), (0, 0), (0, 1), (0, 2), (0, 3))
 PE_TOKENS = 384
 PE_HALVES = ((0, 192), (192, 384))
 LAST = 256
@@ -81,11 +81,7 @@ def tile_routed_moe_kernel(tc, xT, w, gate, offs, pos1, pos2, out):
             xs.append(keep.tile([P, n], U8, name="xs%d" % i, align_bytes=64))
             for j, e in enumerate(experts):
                 where[e] = (i, j * C)
-        acc, bank_of = [], {}
-        for i, experts in enumerate(BANKS):
-            acc.append(psum.tile([P, len(experts) * C], F32, name="acc%d" % i))
-            for j, e in enumerate(experts):
-                bank_of[e] = (i, j * C)
+        acc = [psum.tile([P, b - a], F32, name="acc%d" % a) for a, b in BANKS]
         wc = keep.tile([P, E * N], U32, name="wc", align_bytes=64)
         ws = keep.tile([P, E * N], U8, name="ws", align_bytes=64)
         wg = keep.tile([P, E, N, 4], BF16, name="wg", tag="stage", align_bytes=64)
@@ -100,48 +96,44 @@ def tile_routed_moe_kernel(tc, xT, w, gate, offs, pos1, pos2, out):
 
         def gather(t, e):
             i, c0 = where[e]
-            if (t // 2, e) in SHARED_UNITS:
-                pieces = ((0, C // 2, True), (C // 2, C, False))
+            dst = pairs[i][:, t // 2, c0 : c0 + C, t % 2]
+            entries = offs_t[:, e * C // 16 : (e + 1) * C // 16]
+            if (t // 2, e) in VECTOR_UNITS:
+                nc.vector.tensor_copy(dst, xr[t // 2][:, t % 2, :].indirect(entries))
             else:
-                pieces = ((0, C, (t // 2, e) in VECTOR_UNITS),)
-            for a, b, on_vector in pieces:
-                dst = pairs[i][:, t // 2, c0 + a : c0 + b, t % 2]
-                entries = offs_t[:, (e * C + a) // 16 : (e * C + b) // 16]
-                if on_vector:
-                    nc.vector.tensor_copy(dst, xr[t // 2][:, t % 2, :].indirect(entries))
-                else:
-                    nc.scalar.activation(dst, xb[:, t, :].indirect(entries), COPY)
+                nc.scalar.activation(dst, xb[:, t, :].indirect(entries), COPY)
 
         def interleave_x(i):
-            nc.vector.tensor_copy(
+            copy = nc.scalar.copy if i >= len(GROUPS) - 2 else nc.vector.tensor_copy
+            copy(
                 grouped[i].rearrange("p n t -> p (n t)").bitcast(F32).rearrange("p (n u) -> p n u", u=2),
                 pairs[i][:].rearrange("p u n e -> p (u n e)").bitcast(F32).rearrange("p (u n) -> p n u", u=2),
             )
 
-        def quantise_x(i):
+        def quantise_x(i, a, b):
             nc.vector.quantize_mx(
-                out=xc[i][:].bitcast(FP8X4),
-                scales=xs[i][:],
-                in_=grouped[i].rearrange("p n t -> p (n t)"),
+                out=xc[i][:, a:b].bitcast(FP8X4),
+                scales=xs[i][:, a:b],
+                in_=grouped[i][:, a:b].rearrange("p n t -> p (n t)"),
             )
 
-        def multiply(i):
-            for e in GROUPS[i]:
-                c0 = where[e][1]
-                b, a0 = bank_of[e]
-                nc.tensor.matmul_mx(
-                    out=acc[b][:, a0 : a0 + C],
-                    lhsT=wc[:, e * N : (e + 1) * N].bitcast(FP8X4),
-                    lhsT_scale=ws[:, e * N : (e + 1) * N],
-                    rhs=xc[i][:, c0 : c0 + C].bitcast(FP8X4),
-                    rhs_scale=xs[i][:, c0 : c0 + C],
-                    start=True,
-                    stop=True,
-                )
+        def multiply(e, a, b):
+            i, c0 = where[e]
+            bank = max(k for k in range(len(BANKS)) if BANKS[k][0] <= e * C + a)
+            s0 = BANKS[bank][0]
+            nc.tensor.matmul_mx(
+                out=acc[bank][:, e * C + a - s0 : e * C + b - s0],
+                lhsT=wc[:, e * N : (e + 1) * N].bitcast(FP8X4),
+                lhsT_scale=ws[:, e * N : (e + 1) * N],
+                rhs=xc[i][:, c0 + a : c0 + b].bitcast(FP8X4),
+                rhs_scale=xs[i][:, c0 + a : c0 + b],
+                start=True,
+                stop=True,
+            )
 
         def empty(b):
-            e0 = BANKS[b][0]
-            nc.scalar.copy(y[:, e0 * C : (e0 + len(BANKS[b])) * C], acc[b][:])
+            copy = nc.vector.tensor_copy if b in VECTOR_BANKS else nc.scalar.copy
+            copy(y[:, BANKS[b][0] : BANKS[b][1]], acc[b][:])
 
         cast_plane(2, 0, 512)
         cast_plane(2, 512, 768)
@@ -167,20 +159,22 @@ def tile_routed_moe_kernel(tc, xT, w, gate, offs, pos1, pos2, out):
             wraw[1][:].rearrange("p e j (c i) -> p e c j i", i=4),
         )
         xc[0] = keep.tile([P, 4 * C], U32, name="xc0", tag="raw", align_bytes=64)
-        quantise_x(0)
+        quantise_x(0, 0, 4 * C)
         nc.vector.quantize_mx(out=wc[:].bitcast(FP8X4), scales=ws[:], in_=wg[:].rearrange("p e n j -> p (e n j)"))
         later_groups = keep.tile([P, 4 * C, 4], BF16, name="later_groups", tag="stage", align_bytes=64)
         for experts in GROUPS[1:]:
             a = (experts[0] - 4) * C
             grouped.append(later_groups[:, a : a + len(experts) * C, :])
-        multiply(0)
+        for e in GROUPS[0]:
+            multiply(e, 0, C)
         interleave_x(1)
         for i in range(2, len(GROUPS)):
             interleave_x(i)
-            quantise_x(i - 1)
-            multiply(i - 1)
-        quantise_x(len(GROUPS) - 1)
-        multiply(len(GROUPS) - 1)
+            quantise_x(i - 1, 0, C)
+            multiply(GROUPS[i - 1][0], 0, C)
+        for a, b in ((0, C // 2), (C // 2, C)):
+            quantise_x(len(GROUPS) - 1, a, b)
+            multiply(E - 1, a, b)
         for b in range(len(BANKS)):
             empty(b)
 

from contextlib import ExitStack

import concourse.mybir as mybir
from concourse.masks import make_identity

K, T, E, C, N = 512, 1024, 8, 256, 128
SLOTS = E * C
FLOPS = 2 * K * N * SLOTS

F32 = mybir.dt.float32
BF16 = mybir.dt.bfloat16
U32 = mybir.dt.uint32
U16 = mybir.dt.uint16
U8 = mybir.dt.uint8
FP8X4 = mybir.dt.float8_e4m3fn_x4
MULT = mybir.AluOpType.mult
ADD = mybir.AluOpType.add
COPY = mybir.ActivationFunctionType.Copy

P = 128
GROUPS = ((0, 1, 2, 3), (4,), (5,), (6,), (7,))
BANKS = ((0, 512), (512, 1024), (1024, 1536), (1536, 1792), (1792, 1920), (1920, 2048))
VECTOR_BANKS = (2,)
VECTOR_UNITS = ((1, 0), (1, 1), (0, 0), (0, 1), (0, 2), (0, 3))
PE_TOKENS = 384
PE_HALVES = ((0, 192), (192, 384))
LAST = 256


def tile_routed_moe_kernel(tc, xT, w, gate, offs, pos1, pos2, out):
    nc = tc.nc
    with ExitStack() as ctx:
        lists = ctx.enter_context(tc.tile_pool(name="lists", bufs=1))
        keep = ctx.enter_context(tc.tile_pool(name="keep", bufs=1))
        psum = ctx.enter_context(tc.psum_pool(name="psum", bufs=1))

        offs_t = lists.tile([P, SLOTS // 16], U16, name="offs_t")
        pos1_t = lists.tile([P, T // 16], U16, name="pos1_t")
        pos2_t = lists.tile([P, T // 16], U16, name="pos2_t")

        planes = xT.rearrange("(p t) n -> t p n", t=4)
        xr = [keep.tile([P, 2, T], F32, name="xr%d" % u) for u in range(2)]
        wraw = [
            keep.tile([P, 4, 4, N], F32, name="wraw0", align_bytes=64),
            keep.tile([P, 4, 4, N], F32, name="wraw1", tag="raw", align_bytes=64),
        ]

        def load_w(e0, e1):
            nc.sync.dma_start(wraw[e0 // 4][:, e0 % 4 : e0 % 4 + e1 - e0], w[e0:e1].rearrange("e (p j) n -> p e j n", j=4))

        for t, n0, n1 in ((2, 0, 512), (2, 512, 1024), (3, 0, 512), (3, 512, 1024), (0, 0, 1024), (1, 0, 1024)):
            if t == 1:
                load_w(0, 2)
            nc.sync.dma_start(xr[t // 2][:, t % 2, n0:n1], planes[t][:, n0:n1])
            if (t, n1) == (2, T):
                nc.sync.dma_start(offs_t[:], offs)
        load_w(2, 4)
        load_w(4, 8)
        nc.sync.dma_start(pos1_t[:], pos1)
        nc.sync.dma_start(pos2_t[:], pos2)
        gate_t = []
        for r in range(2):
            g = keep.tile([P, T], F32, name="gate%d" % r)
            nc.sync.dma_start(g[:], gate[r])
            gate_t.append(g)

        warm_a = keep.tile([P, 1], F32, name="warm_a")
        warm_b = keep.tile([P, 1], F32, name="warm_b")
        nc.vector.memset(warm_a[:], 0.0)
        nc.scalar.copy(warm_b[:], warm_a[:])
        identity = keep.tile([P, P], F32, name="identity")
        make_identity(nc, identity[:])

        xb = keep.tile([P, 4, T], BF16, name="xb")
        pairs, xc, xs, where = [], {}, [], {}
        for i, experts in enumerate(GROUPS):
            n = len(experts) * C
            pairs.append(keep.tile([P, 2, n, 2], BF16, name="pairs%d" % i, align_bytes=64))
            if i > 0:
                xc[i] = keep.tile([P, n], U32, name="xc%d" % i, align_bytes=64)
            xs.append(keep.tile([P, n], U8, name="xs%d" % i, align_bytes=64))
            for j, e in enumerate(experts):
                where[e] = (i, j * C)
        acc = [psum.tile([P, b - a], F32, name="acc%d" % a) for a, b in BANKS]
        wc = keep.tile([P, E * N], U32, name="wc", align_bytes=64)
        ws = keep.tile([P, E * N], U8, name="ws", align_bytes=64)
        wg = keep.tile([P, E, N, 4], BF16, name="wg", tag="stage", align_bytes=64)
        y = keep.tile([P, SLOTS], F32, name="y")
        grouped = []

        def cast_plane(t, n0, n1):
            if t == 2:
                nc.scalar.copy(xb[:, t, n0:n1], xr[t // 2][:, t % 2, n0:n1])
            else:
                nc.gpsimd.tensor_copy(xb[:, t, n0:n1], xr[t // 2][:, t % 2, n0:n1])

        def gather(t, e):
            i, c0 = where[e]
            dst = pairs[i][:, t // 2, c0 : c0 + C, t % 2]
            entries = offs_t[:, e * C // 16 : (e + 1) * C // 16]
            if (t // 2, e) in VECTOR_UNITS:
                nc.vector.tensor_copy(dst, xr[t // 2][:, t % 2, :].indirect(entries))
            else:
                nc.scalar.activation(dst, xb[:, t, :].indirect(entries), COPY)

        def interleave_x(i):
            copy = nc.scalar.copy if i >= len(GROUPS) - 2 else nc.vector.tensor_copy
            copy(
                grouped[i].rearrange("p n t -> p (n t)").bitcast(F32).rearrange("p (n u) -> p n u", u=2),
                pairs[i][:].rearrange("p u n e -> p (u n e)").bitcast(F32).rearrange("p (u n) -> p n u", u=2),
            )

        def quantise_x(i, a, b):
            nc.vector.quantize_mx(
                out=xc[i][:, a:b].bitcast(FP8X4),
                scales=xs[i][:, a:b],
                in_=grouped[i][:, a:b].rearrange("p n t -> p (n t)"),
            )

        def multiply(e, a, b):
            i, c0 = where[e]
            bank = max(k for k in range(len(BANKS)) if BANKS[k][0] <= e * C + a)
            s0 = BANKS[bank][0]
            nc.tensor.matmul_mx(
                out=acc[bank][:, e * C + a - s0 : e * C + b - s0],
                lhsT=wc[:, e * N : (e + 1) * N].bitcast(FP8X4),
                lhsT_scale=ws[:, e * N : (e + 1) * N],
                rhs=xc[i][:, c0 + a : c0 + b].bitcast(FP8X4),
                rhs_scale=xs[i][:, c0 + a : c0 + b],
                start=True,
                stop=True,
            )

        def empty(b):
            copy = nc.vector.tensor_copy if b in VECTOR_BANKS else nc.scalar.copy
            copy(y[:, BANKS[b][0] : BANKS[b][1]], acc[b][:])

        cast_plane(2, 0, 512)
        cast_plane(2, 512, 768)
        nc.vector.tensor_copy(xb[:, 2, 768:T], xr[1][:, 0, 768:T])
        def copy_w(e):
            nc.gpsimd.tensor_copy(wg[:, e : e + 2], wraw[0][:, e : e + 2].rearrange("p e j n -> p e n j"))

        for n0 in range(0, T, 512):
            cast_plane(3, n0, n0 + 512)
        cast_plane(0, 0, 1024)
        copy_w(0)
        cast_plane(1, 0, 1024)
        copy_w(2)
        for t in (2, 3, 0, 1):
            for e in range(8):
                gather(t, e)

        first_group = keep.tile([P, 4 * C, 4], BF16, name="first_group", align_bytes=64)
        grouped.append(first_group[:])
        interleave_x(0)
        nc.vector.tensor_copy(
            wg[:, 4:8].rearrange("p e (c i) j -> p e c j i", i=4),
            wraw[1][:].rearrange("p e j (c i) -> p e c j i", i=4),
        )
        xc[0] = keep.tile([P, 4 * C], U32, name="xc0", tag="raw", align_bytes=64)
        quantise_x(0, 0, 4 * C)
        nc.vector.quantize_mx(out=wc[:].bitcast(FP8X4), scales=ws[:], in_=wg[:].rearrange("p e n j -> p (e n j)"))
        later_groups = keep.tile([P, 4 * C, 4], BF16, name="later_groups", tag="stage", align_bytes=64)
        for experts in GROUPS[1:]:
            a = (experts[0] - 4) * C
            grouped.append(later_groups[:, a : a + len(experts) * C, :])
        for e in GROUPS[0]:
            multiply(e, 0, C)
        interleave_x(1)
        for i in range(2, len(GROUPS)):
            interleave_x(i)
            quantise_x(i - 1, 0, C)
            multiply(GROUPS[i - 1][0], 0, C)
        for a, b in ((0, C // 2), (C // 2, C)):
            quantise_x(len(GROUPS) - 1, a, b)
            multiply(E - 1, a, b)
        for b in range(len(BANKS)):
            empty(b)

        first = keep.tile([P, T], F32, name="first")
        second = keep.tile([P, T], F32, name="second")
        total = keep.tile([P, T], F32, name="total")
        sums = [psum.tile([P, b - a], F32, name="sums%d" % a) for a, b in PE_HALVES]

        def fetch(dst, pos_t, r, a, b):
            nc.vector.tensor_tensor(dst[:, a:b], y[:].indirect(pos_t[:, a // 16 : b // 16]), gate_t[r][:, a:b], MULT)

        def add_and_store(a, b):
            nc.vector.tensor_tensor(total[:, a:b], first[:, a:b], second[:, a:b], ADD)
            nc.sync.dma_start(out[:, a:b], total[:, a:b])

        fetch(first, pos1_t, 0, 0, PE_TOKENS)
        fetch(second, pos2_t, 1, 0, PE_TOKENS)
        for half, (a, b) in zip(sums, PE_HALVES):
            nc.tensor.matmul(half[:], identity[:], first[:, a:b], start=True, stop=False)
        for half, (a, b) in zip(sums, PE_HALVES):
            nc.tensor.matmul(half[:], identity[:], second[:, a:b], start=False, stop=True)
            nc.scalar.copy(total[:, a:b], half[:])
            nc.scalar.dma_start(out[:, a:b], total[:, a:b])
        fetch(first, pos1_t, 0, PE_TOKENS, T)
        fetch(second, pos2_t, 1, PE_TOKENS, T - LAST)
        fetch(second, pos2_t, 1, T - LAST, T)
        add_and_store(PE_TOKENS, T - LAST)
        add_and_store(T - LAST, T)
